import numpy as np
import ml_dtypes

BF16 = ml_dtypes.bfloat16


def bf(x):
    return np.asarray(x, np.float32).astype(BF16)


def f32(x):
    return np.asarray(x, np.float32)


def f64(x):
    return np.asarray(x).astype(np.float64)


def striped(idx):
    return np.tile(idx.reshape(-1, 16).T, (8, 1))


S, K, M, N = 2048, 128, 128, 1024


def setup_inputs():
    return {"table": bf(np.random.standard_normal((S, K))), "w": bf(np.random.standard_normal((K, M)) / np.sqrt(K)), "b": f32(0.5 * np.random.standard_normal((M, 1))), "offs": striped(np.random.permutation(np.tile(np.arange(S), 2))[:N])}


def reference(table, w, b, offs):
    idx = offs[:16].T.reshape(-1)
    x = f64(table)[idx].T
    y = f64(w).T @ x
    return np.tanh(y + f64(b))

@@ -1,0 +1,57 @@
+import concourse.mybir as mybir
+from concourse.masks import make_identity
+
+BF16, F32, U16 = mybir.dt.bfloat16, mybir.dt.float32, mybir.dt.uint16
+TANH = mybir.ActivationFunctionType.Tanh
+
+P = 128
+WORDS = 2048
+TOKENS = 1024
+BLOCKS = WORDS // P
+GROUP = 4
+PIECE = 512
+
+FLOPS = 2 * P * P * TOKENS
+
+
+def tile_gather_matmul_kernel(tc, table, w, b, offs, out):
+    nc = tc.nc
+    with (
+        tc.tile_pool(name="held", bufs=1) as held,
+        tc.tile_pool(name="results", bufs=2) as results,
+        tc.psum_pool(name="flips", bufs=2) as flips,
+        tc.psum_pool(name="products", bufs=2) as products,
+    ):
+        offsets = held.tile([P, TOKENS // 16], U16, name="offsets")
+        nc.sync.dma_start(offsets[:], offs)
+
+        identity = held.tile([P, P], BF16, name="identity")
+        make_identity(nc, identity[:])
+
+        blocked = table.rearrange("(a p) k -> p a k", p=P)
+        rows = []
+        for g in range(BLOCKS // GROUP):
+            rows_g = held.tile([P, GROUP, P], BF16, name="rows%d" % g)
+            queue = nc.sync if g % 2 == 0 else nc.scalar
+            queue.dma_start(rows_g[:], blocked[:, g * GROUP : (g + 1) * GROUP, :])
+            rows.append(rows_g)
+
+        weights = held.tile([P, P], BF16, name="weights")
+        nc.gpsimd.dma_start(weights[:], w)
+        bias = held.tile([P, 1], F32, name="bias")
+        nc.gpsimd.dma_start(bias[:], b)
+
+        words = held.tile([P, WORDS], BF16, name="words")
+        for g in range(BLOCKS // GROUP):
+            flipped = flips.tile([P, GROUP * P], BF16, name="flipped")
+            for a in range(GROUP):
+                nc.tensor.transpose(flipped[:, a * P : (a + 1) * P], rows[g][:, a, :], identity[:])
+            nc.vector.tensor_copy(words[:, g * GROUP * P : (g + 1) * GROUP * P], flipped[:])
+
+        for piece in range(TOKENS // PIECE):
+            picked = words[:].indirect(offsets[:, piece * (PIECE // 16) : (piece + 1) * (PIECE // 16)])
+            product = products.tile([P, PIECE], F32, name="product")
+            nc.tensor.matmul(product[:], weights[:], picked, start=True, stop=True)
+            result = results.tile([P, PIECE], F32, name="result")
+            nc.scalar.activation(result[:], product[:], TANH, bias=bias[:, 0:1])
+            nc.sync.dma_start(out[:, piece * PIECE : (piece + 1) * PIECE], result[:])

@@ -7,9 +7,9 @@ TANH = mybir.ActivationFunctionType.Tanh
 P = 128
 WORDS = 2048
 TOKENS = 1024
-BLOCKS = WORDS // P
-GROUP = 4
-PIECE = 512
+PIECE = 256
+ROWS = 4
+CHUNK = P * ROWS
 
 FLOPS = 2 * P * P * TOKENS
 
@@ -18,35 +18,44 @@ def tile_gather_matmul_kernel(tc, table, w, b, offs, out):
     nc = tc.nc
     with (
         tc.tile_pool(name="held", bufs=1) as held,
-        tc.tile_pool(name="results", bufs=2) as results,
-        tc.psum_pool(name="flips", bufs=2) as flips,
-        tc.psum_pool(name="products", bufs=2) as products,
+        tc.tile_pool(name="results", bufs=4) as results,
+        tc.psum_pool(name="flips", bufs=4) as flips,
+        tc.psum_pool(name="products", bufs=4) as products,
     ):
+        loaded = []
+        for chunk in range(WORDS // CHUNK):
+            rows = held.tile([P, ROWS * P], BF16, name="rows%d" % chunk)
+            queue = nc.sync if chunk % 2 == 0 else nc.scalar
+            queue.dma_start(
+                rows[:], table[chunk * CHUNK : (chunk + 1) * CHUNK, :].rearrange("(p r) k -> p (r k)", r=ROWS)
+            )
+            loaded.append(rows)
+
         offsets = held.tile([P, TOKENS // 16], U16, name="offsets")
         nc.sync.dma_start(offsets[:], offs)
+        weights = held.tile([P, P], BF16, name="weights")
+        nc.sync.dma_start(weights[:], w)
+        bias = held.tile([P, 1], F32, name="bias")
+        nc.sync.dma_start(bias[:], b)
 
         identity = held.tile([P, P], BF16, name="identity")
         make_identity(nc, identity[:])
 
-        blocked = table.rearrange("(a p) k -> p a k", p=P)
-        rows = []
-        for g in range(BLOCKS // GROUP):
-            rows_g = held.tile([P, GROUP, P], BF16, name="rows%d" % g)
-            queue = nc.sync if g % 2 == 0 else nc.scalar
-            queue.dma_start(rows_g[:], blocked[:, g * GROUP : (g + 1) * GROUP, :])
-            rows.append(rows_g)
-
-        weights = held.tile([P, P], BF16, name="weights")
-        nc.gpsimd.dma_start(weights[:], w)
-        bias = held.tile([P, 1], F32, name="bias")
-        nc.gpsimd.dma_start(bias[:], b)
+        scratch = held.tile([P, 1], F32, name="scratch")
+        nc.vector.memset(scratch[:], 0.0)
+        nc.scalar.activation(scratch[:], scratch[:], TANH)
 
         words = held.tile([P, WORDS], BF16, name="words")
-        for g in range(BLOCKS // GROUP):
-            flipped = flips.tile([P, GROUP * P], BF16, name="flipped")
-            for a in range(GROUP):
-                nc.tensor.transpose(flipped[:, a * P : (a + 1) * P], rows[g][:, a, :], identity[:])
-            nc.vector.tensor_copy(words[:, g * GROUP * P : (g + 1) * GROUP * P], flipped[:])
+        for chunk in range(WORDS // CHUNK):
+            flipped = flips.tile([P, CHUNK], BF16, name="flipped")
+            for r in range(ROWS):
+                nc.tensor.transpose(flipped[:, r * P : (r + 1) * P], loaded[chunk][:, r * P : (r + 1) * P], identity[:])
+            in_order = flipped[:].rearrange("k (r p) -> k p r", r=ROWS)
+            columns = words[:, chunk * CHUNK : (chunk + 1) * CHUNK].rearrange("k (p r) -> k p r", r=ROWS)
+            if chunk % 2 == 0:
+                nc.vector.tensor_copy(columns, in_order)
+            else:
+                nc.scalar.copy(columns, in_order)
 
         for piece in range(TOKENS // PIECE):
             picked = words[:].indirect(offsets[:, piece * (PIECE // 16) : (piece + 1) * (PIECE // 16)])

@@ -10,6 +10,8 @@ TOKENS = 1024
 PIECE = 256
 ROWS = 4
 CHUNK = P * ROWS
+BANK = 512
+WARM_UPS = 3
 
 FLOPS = 2 * P * P * TOKENS
 
@@ -19,8 +21,9 @@ def tile_gather_matmul_kernel(tc, table, w, b, offs, out):
     with (
         tc.tile_pool(name="held", bufs=1) as held,
         tc.tile_pool(name="results", bufs=4) as results,
-        tc.psum_pool(name="flips", bufs=4) as flips,
+        tc.psum_pool(name="flips", bufs=3) as flips,
         tc.psum_pool(name="products", bufs=4) as products,
+        tc.psum_pool(name="unread", bufs=1) as unread,
     ):
         loaded = []
         for chunk in range(WORDS // CHUNK):
@@ -44,6 +47,12 @@ def tile_gather_matmul_kernel(tc, table, w, b, offs, out):
         scratch = held.tile([P, 1], F32, name="scratch")
         nc.vector.memset(scratch[:], 0.0)
         nc.scalar.activation(scratch[:], scratch[:], TANH)
+
+        zeros = held.tile([P, BANK], BF16, name="zeros")
+        nc.vector.memset(zeros[:], 0.0)
+        nothing = unread.tile([P, BANK], F32, name="nothing")
+        for warm_up in range(WARM_UPS):
+            nc.tensor.matmul(nothing[:], zeros[:, 0:P], zeros[:], start=True, stop=True)
 
         words = held.tile([P, WORDS], BF16, name="words")
         for chunk in range(WORDS // CHUNK):

import concourse.mybir as mybir
from concourse.masks import make_identity

BF16, F32, U16 = mybir.dt.bfloat16, mybir.dt.float32, mybir.dt.uint16
TANH = mybir.ActivationFunctionType.Tanh

P = 128
WORDS = 2048
TOKENS = 1024
PIECE = 256
ROWS = 4
CHUNK = P * ROWS
BANK = 512
WARM_UPS = 3

FLOPS = 2 * P * P * TOKENS


def tile_gather_matmul_kernel(tc, table, w, b, offs, out):
    nc = tc.nc
    with (
        tc.tile_pool(name="held", bufs=1) as held,
        tc.tile_pool(name="results", bufs=4) as results,
        tc.psum_pool(name="flips", bufs=3) as flips,
        tc.psum_pool(name="products", bufs=4) as products,
        tc.psum_pool(name="unread", bufs=1) as unread,
    ):
        loaded = []
        for chunk in range(WORDS // CHUNK):
            rows = held.tile([P, ROWS * P], BF16, name="rows%d" % chunk)
            queue = nc.sync if chunk % 2 == 0 else nc.scalar
            queue.dma_start(
                rows[:], table[chunk * CHUNK : (chunk + 1) * CHUNK, :].rearrange("(p r) k -> p (r k)", r=ROWS)
            )
            loaded.append(rows)

        offsets = held.tile([P, TOKENS // 16], U16, name="offsets")
        nc.sync.dma_start(offsets[:], offs)
        weights = held.tile([P, P], BF16, name="weights")
        nc.sync.dma_start(weights[:], w)
        bias = held.tile([P, 1], F32, name="bias")
        nc.sync.dma_start(bias[:], b)

        identity = held.tile([P, P], BF16, name="identity")
        make_identity(nc, identity[:])

        scratch = held.tile([P, 1], F32, name="scratch")
        nc.vector.memset(scratch[:], 0.0)
        nc.scalar.activation(scratch[:], scratch[:], TANH)

        zeros = held.tile([P, BANK], BF16, name="zeros")
        nc.vector.memset(zeros[:], 0.0)
        nothing = unread.tile([P, BANK], F32, name="nothing")
        for warm_up in range(WARM_UPS):
            nc.tensor.matmul(nothing[:], zeros[:, 0:P], zeros[:], start=True, stop=True)

        words = held.tile([P, WORDS], BF16, name="words")
        for chunk in range(WORDS // CHUNK):
            flipped = flips.tile([P, CHUNK], BF16, name="flipped")
            for r in range(ROWS):
                nc.tensor.transpose(flipped[:, r * P : (r + 1) * P], loaded[chunk][:, r * P : (r + 1) * P], identity[:])
            in_order = flipped[:].rearrange("k (r p) -> k p r", r=ROWS)
            columns = words[:, chunk * CHUNK : (chunk + 1) * CHUNK].rearrange("k (p r) -> k p r", r=ROWS)
            if chunk % 2 == 0:
                nc.vector.tensor_copy(columns, in_order)
            else:
                nc.scalar.copy(columns, in_order)

        for piece in range(TOKENS // PIECE):
            picked = words[:].indirect(offsets[:, piece * (PIECE // 16) : (piece + 1) * (PIECE // 16)])
            product = products.tile([P, PIECE], F32, name="product")
            nc.tensor.matmul(product[:], weights[:], picked, start=True, stop=True)
            result = results.tile([P, PIECE], F32, name="result")
            nc.scalar.activation(result[:], product[:], TANH, bias=bias[:, 0:1])
            nc.sync.dma_start(out[:, piece * PIECE : (piece + 1) * PIECE], result[:])
